import numpy as np
import ml_dtypes

BF16 = ml_dtypes.bfloat16


def bf(x):
    return np.asarray(x, np.float32).astype(BF16)


def f32(x):
    return np.asarray(x, np.float32)


def f64(x):
    return np.asarray(x).astype(np.float64)


def striped(idx):
    return np.concatenate([l.reshape(-1, 16).T for l in idx])


def rows(idx, k):
    return np.tile(np.repeat(idx, 16, axis=0), (k // (16 * 8), 1))


def look(tab, idx):
    return np.take_along_axis(f64(tab), rows(idx, len(tab)), axis=1)


P, K, S, V, N = 128, 512, 2048, 1536, 1536


def setup_inputs():
    return {"tab": f32(0.5 * np.random.standard_normal((K, S))), "u": f32(0.3 * np.random.standard_normal((K, V))), "e": bf(np.tile(np.eye(16), (8, 1))), "bj": f32(np.random.standard_normal((1, V))), "offs": striped(np.random.randint(0, S, (8, N)))}


def reference(tab, u, e, bj, offs):
    idx = np.stack([g.T.reshape(-1) for g in np.split(offs, 8)])
    s = look(tab, idx) + f64(u)
    s = np.concatenate([f64(e).T @ s[a:a + P] for a in range(0, K, P)])
    x = s + f64(bj)
    return x

@@ -1,0 +1,63 @@
+import concourse.mybir as mybir
+
+F32, BF16, U16 = mybir.dt.float32, mybir.dt.bfloat16, mybir.dt.uint16
+ADD = mybir.AluOpType.add
+
+P = 128
+ROWS, COLUMNS = 512, 2048
+VECTORS = 1536
+BLOCKS = ROWS // P
+QUERIES = 16
+OUT_ROWS = BLOCKS * QUERIES
+PIECE = 512
+PIECES = VECTORS // PIECE
+LIST_COLUMNS = PIECE // 16
+FLOPS = ROWS * VECTORS * 3
+
+
+def tile_lookup_adc_bias_out_kernel(tc, tab, u, e, bj, offs, out):
+    nc = tc.nc
+    with (
+        tc.tile_pool(name="held", bufs=1) as held,
+        tc.psum_pool(name="psum", bufs=1) as psum,
+    ):
+        offsets = held.tile([P, VECTORS // 16], U16, name="offsets")
+        nc.sync.dma_start(offsets[:], offs)
+
+        middle = OUT_ROWS - QUERIES
+        spread = held.tile([P, 2 * middle + QUERIES], BF16, name="spread")
+        nc.gpsimd.memset(spread[:], 0.0)
+        nc.scalar.dma_start(spread[:, middle : middle + QUERIES], e)
+
+        tables = []
+        corrections = []
+        for b in range(BLOCKS):
+            rows = slice(b * P, (b + 1) * P)
+            table = held.tile([P, COLUMNS], F32, name=f"table{b}")
+            nc.sync.dma_start(table[:], tab[rows, :])
+            tables.append(table)
+            for c in range(PIECES):
+                correction = held.tile([P, PIECE], F32, name=f"correction{b}_{c}")
+                nc.sync.dma_start(correction[:], u[rows, c * PIECE : (c + 1) * PIECE])
+                corrections.append(correction)
+        bias = held.tile([OUT_ROWS, VECTORS], F32, name="bias")
+        nc.sync.dma_start(bias[:], bj[0, :].partition_broadcast(OUT_ROWS))
+
+        scores = [psum.tile([OUT_ROWS, PIECE], F32, name=f"scores{c}") for c in range(PIECES)]
+        for b in range(BLOCKS):
+            weights = spread[:, middle - b * QUERIES : middle - b * QUERIES + OUT_ROWS]
+            for c in range(PIECES):
+                piece_offsets = offsets[:, c * LIST_COLUMNS : (c + 1) * LIST_COLUMNS]
+                summed = held.tile([P, PIECE], F32, name=f"summed{b}_{c}")
+                nc.vector.tensor_tensor(
+                    summed[:], tables[b][:].indirect(piece_offsets), corrections[b * PIECES + c][:], ADD
+                )
+                rounded = held.tile([P, PIECE], BF16, name=f"rounded{b}_{c}")
+                nc.scalar.copy(rounded[:], summed[:])
+                nc.tensor.matmul(scores[c][:], weights, rounded[:], start=(b == 0), stop=(b == BLOCKS - 1))
+
+        for c in range(PIECES):
+            columns = slice(c * PIECE, (c + 1) * PIECE)
+            biased = held.tile([OUT_ROWS, PIECE], F32, name=f"biased{c}")
+            nc.vector.tensor_tensor(biased[:], scores[c][:], bias[:, columns], ADD)
+            nc.sync.dma_start(out[:, columns], biased[:])

@@ -11,6 +11,8 @@ QUERIES = 16
 OUT_ROWS = BLOCKS * QUERIES
 PIECE = 512
 PIECES = VECTORS // PIECE
+STEP = PIECE // 2
+STEPS = VECTORS // STEP
 LIST_COLUMNS = PIECE // 16
 FLOPS = ROWS * VECTORS * 3
 
@@ -30,34 +32,38 @@ def tile_lookup_adc_bias_out_kernel(tc, tab, u, e, bj, offs, out):
         nc.scalar.dma_start(spread[:, middle : middle + QUERIES], e)
 
         tables = []
-        corrections = []
+        firsts = []
+        rests = []
         for b in range(BLOCKS):
             rows = slice(b * P, (b + 1) * P)
             table = held.tile([P, COLUMNS], F32, name=f"table{b}")
             nc.sync.dma_start(table[:], tab[rows, :])
             tables.append(table)
-            for c in range(PIECES):
-                correction = held.tile([P, PIECE], F32, name=f"correction{b}_{c}")
-                nc.sync.dma_start(correction[:], u[rows, c * PIECE : (c + 1) * PIECE])
-                corrections.append(correction)
+            first = held.tile([P, PIECE], F32, name=f"first{b}")
+            nc.sync.dma_start(first[:], u[rows, :PIECE])
+            firsts.append(first)
+            rest = held.tile([P, VECTORS - PIECE], F32, name=f"rest{b}")
+            nc.sync.dma_start(rest[:], u[rows, PIECE:])
+            rests.append(rest)
         bias = held.tile([OUT_ROWS, VECTORS], F32, name="bias")
         nc.sync.dma_start(bias[:], bj[0, :].partition_broadcast(OUT_ROWS))
 
-        scores = [psum.tile([OUT_ROWS, PIECE], F32, name=f"scores{c}") for c in range(PIECES)]
+        scores = [psum.tile([OUT_ROWS, STEP], F32, name=f"scores{k}") for k in range(STEPS)]
         for b in range(BLOCKS):
             weights = spread[:, middle - b * QUERIES : middle - b * QUERIES + OUT_ROWS]
             for c in range(PIECES):
-                piece_offsets = offsets[:, c * LIST_COLUMNS : (c + 1) * LIST_COLUMNS]
+                correction = firsts[b][:] if c == 0 else rests[b][:, (c - 1) * PIECE : c * PIECE]
                 summed = held.tile([P, PIECE], F32, name=f"summed{b}_{c}")
-                nc.vector.tensor_tensor(
-                    summed[:], tables[b][:].indirect(piece_offsets), corrections[b * PIECES + c][:], ADD
-                )
-                rounded = held.tile([P, PIECE], BF16, name=f"rounded{b}_{c}")
-                nc.scalar.copy(rounded[:], summed[:])
-                nc.tensor.matmul(scores[c][:], weights, rounded[:], start=(b == 0), stop=(b == BLOCKS - 1))
+                piece_offsets = offsets[:, c * LIST_COLUMNS : (c + 1) * LIST_COLUMNS]
+                nc.vector.tensor_tensor(summed[:], tables[b][:].indirect(piece_offsets), correction, ADD)
+                for h in range(PIECE // STEP):
+                    rounded = held.tile([P, STEP], BF16, name=f"rounded{b}_{c}_{h}")
+                    nc.scalar.copy(rounded[:], summed[:, h * STEP : (h + 1) * STEP])
+                    step_scores = scores[c * (PIECE // STEP) + h]
+                    nc.tensor.matmul(step_scores[:], weights, rounded[:], start=(b == 0), stop=(b == BLOCKS - 1))
 
-        for c in range(PIECES):
-            columns = slice(c * PIECE, (c + 1) * PIECE)
-            biased = held.tile([OUT_ROWS, PIECE], F32, name=f"biased{c}")
-            nc.vector.tensor_tensor(biased[:], scores[c][:], bias[:, columns], ADD)
+        for k in range(STEPS):
+            columns = slice(k * STEP, (k + 1) * STEP)
+            biased = held.tile([OUT_ROWS, STEP], F32, name=f"biased{k}")
+            nc.vector.tensor_tensor(biased[:], scores[k][:], bias[:, columns], ADD)
             nc.sync.dma_start(out[:, columns], biased[:])

@@ -13,6 +13,7 @@ PIECE = 512
 PIECES = VECTORS // PIECE
 STEP = PIECE // 2
 STEPS = VECTORS // STEP
+BIAS_ROWS = 32
 LIST_COLUMNS = PIECE // 16
 FLOPS = ROWS * VECTORS * 3
 
@@ -31,6 +32,12 @@ def tile_lookup_adc_bias_out_kernel(tc, tab, u, e, bj, offs, out):
         nc.gpsimd.memset(spread[:], 0.0)
         nc.scalar.dma_start(spread[:, middle : middle + QUERIES], e)
 
+        ones = held.tile([BIAS_ROWS, P], F32, name="ones")
+        nc.gpsimd.memset(ones[:], 0.0)
+        nc.gpsimd.memset(ones[:1, :], 1.0)
+        bias = held.tile([BIAS_ROWS, VECTORS], F32, name="bias")
+        nc.vector.memset(bias[:], 0.0)
+
         tables = []
         firsts = []
         rests = []
@@ -42,13 +49,14 @@ def tile_lookup_adc_bias_out_kernel(tc, tab, u, e, bj, offs, out):
             first = held.tile([P, PIECE], F32, name=f"first{b}")
             nc.sync.dma_start(first[:], u[rows, :PIECE])
             firsts.append(first)
+            if b == 0:
+                nc.sync.dma_start(bias[:1, :], bj)
             rest = held.tile([P, VECTORS - PIECE], F32, name=f"rest{b}")
             nc.sync.dma_start(rest[:], u[rows, PIECE:])
             rests.append(rest)
-        bias = held.tile([OUT_ROWS, VECTORS], F32, name="bias")
-        nc.sync.dma_start(bias[:], bj[0, :].partition_broadcast(OUT_ROWS))
-
-        scores = [psum.tile([OUT_ROWS, STEP], F32, name=f"scores{k}") for k in range(STEPS)]
+        scores = [psum.tile([P, STEP], F32, name=f"scores{k}") for k in range(STEPS)]
+        for k in range(STEPS):
+            nc.tensor.matmul(scores[k][:], ones[:], bias[:, k * STEP : (k + 1) * STEP], start=True, stop=False)
         for b in range(BLOCKS):
             weights = spread[:, middle - b * QUERIES : middle - b * QUERIES + OUT_ROWS]
             for c in range(PIECES):
@@ -58,12 +66,18 @@ def tile_lookup_adc_bias_out_kernel(tc, tab, u, e, bj, offs, out):
                 nc.vector.tensor_tensor(summed[:], tables[b][:].indirect(piece_offsets), correction, ADD)
                 for h in range(PIECE // STEP):
                     rounded = held.tile([P, STEP], BF16, name=f"rounded{b}_{c}_{h}")
-                    nc.scalar.copy(rounded[:], summed[:, h * STEP : (h + 1) * STEP])
+                    if (b, c, h) == (BLOCKS - 1, PIECES - 1, 0):
+                        nc.vector.tensor_copy(rounded[:], summed[:, h * STEP : (h + 1) * STEP])
+                    else:
+                        nc.scalar.copy(rounded[:], summed[:, h * STEP : (h + 1) * STEP])
                     step_scores = scores[c * (PIECE // STEP) + h]
-                    nc.tensor.matmul(step_scores[:], weights, rounded[:], start=(b == 0), stop=(b == BLOCKS - 1))
+                    nc.tensor.matmul(step_scores[:OUT_ROWS, :], weights, rounded[:], start=False, stop=(b == BLOCKS - 1))
 
         for k in range(STEPS):
             columns = slice(k * STEP, (k + 1) * STEP)
-            biased = held.tile([OUT_ROWS, STEP], F32, name=f"biased{k}")
-            nc.vector.tensor_tensor(biased[:], scores[k][:], bias[:, columns], ADD)
-            nc.sync.dma_start(out[:, columns], biased[:])
+            stored = held.tile([OUT_ROWS, STEP], F32, name=f"stored{k}")
+            if k % 2 == 0:
+                nc.vector.tensor_copy(stored[:], scores[k][:OUT_ROWS, :])
+            else:
+                nc.scalar.copy(stored[:], scores[k][:OUT_ROWS, :])
+            nc.sync.dma_start(out[:, columns], stored[:])

import concourse.mybir as mybir

F32, BF16, U16 = mybir.dt.float32, mybir.dt.bfloat16, mybir.dt.uint16
ADD = mybir.AluOpType.add

P = 128
ROWS, COLUMNS = 512, 2048
VECTORS = 1536
BLOCKS = ROWS // P
QUERIES = 16
OUT_ROWS = BLOCKS * QUERIES
PIECE = 512
PIECES = VECTORS // PIECE
STEP = PIECE // 2
STEPS = VECTORS // STEP
BIAS_ROWS = 32
LIST_COLUMNS = PIECE // 16
FLOPS = ROWS * VECTORS * 3


def tile_lookup_adc_bias_out_kernel(tc, tab, u, e, bj, offs, out):
    nc = tc.nc
    with (
        tc.tile_pool(name="held", bufs=1) as held,
        tc.psum_pool(name="psum", bufs=1) as psum,
    ):
        offsets = held.tile([P, VECTORS // 16], U16, name="offsets")
        nc.sync.dma_start(offsets[:], offs)

        middle = OUT_ROWS - QUERIES
        spread = held.tile([P, 2 * middle + QUERIES], BF16, name="spread")
        nc.gpsimd.memset(spread[:], 0.0)
        nc.scalar.dma_start(spread[:, middle : middle + QUERIES], e)

        ones = held.tile([BIAS_ROWS, P], F32, name="ones")
        nc.gpsimd.memset(ones[:], 0.0)
        nc.gpsimd.memset(ones[:1, :], 1.0)
        bias = held.tile([BIAS_ROWS, VECTORS], F32, name="bias")
        nc.vector.memset(bias[:], 0.0)

        tables = []
        firsts = []
        rests = []
        for b in range(BLOCKS):
            rows = slice(b * P, (b + 1) * P)
            table = held.tile([P, COLUMNS], F32, name=f"table{b}")
            nc.sync.dma_start(table[:], tab[rows, :])
            tables.append(table)
            first = held.tile([P, PIECE], F32, name=f"first{b}")
            nc.sync.dma_start(first[:], u[rows, :PIECE])
            firsts.append(first)
            if b == 0:
                nc.sync.dma_start(bias[:1, :], bj)
            rest = held.tile([P, VECTORS - PIECE], F32, name=f"rest{b}")
            nc.sync.dma_start(rest[:], u[rows, PIECE:])
            rests.append(rest)
        scores = [psum.tile([P, STEP], F32, name=f"scores{k}") for k in range(STEPS)]
        for k in range(STEPS):
            nc.tensor.matmul(scores[k][:], ones[:], bias[:, k * STEP : (k + 1) * STEP], start=True, stop=False)
        for b in range(BLOCKS):
            weights = spread[:, middle - b * QUERIES : middle - b * QUERIES + OUT_ROWS]
            for c in range(PIECES):
                correction = firsts[b][:] if c == 0 else rests[b][:, (c - 1) * PIECE : c * PIECE]
                summed = held.tile([P, PIECE], F32, name=f"summed{b}_{c}")
                piece_offsets = offsets[:, c * LIST_COLUMNS : (c + 1) * LIST_COLUMNS]
                nc.vector.tensor_tensor(summed[:], tables[b][:].indirect(piece_offsets), correction, ADD)
                for h in range(PIECE // STEP):
                    rounded = held.tile([P, STEP], BF16, name=f"rounded{b}_{c}_{h}")
                    if (b, c, h) == (BLOCKS - 1, PIECES - 1, 0):
                        nc.vector.tensor_copy(rounded[:], summed[:, h * STEP : (h + 1) * STEP])
                    else:
                        nc.scalar.copy(rounded[:], summed[:, h * STEP : (h + 1) * STEP])
                    step_scores = scores[c * (PIECE // STEP) + h]
                    nc.tensor.matmul(step_scores[:OUT_ROWS, :], weights, rounded[:], start=False, stop=(b == BLOCKS - 1))

        for k in range(STEPS):
            columns = slice(k * STEP, (k + 1) * STEP)
            stored = held.tile([OUT_ROWS, STEP], F32, name=f"stored{k}")
            if k % 2 == 0:
                nc.vector.tensor_copy(stored[:], scores[k][:OUT_ROWS, :])
            else:
                nc.scalar.copy(stored[:], scores[k][:OUT_ROWS, :])
            nc.sync.dma_start(out[:, columns], stored[:])
